import numpy as np
import ml_dtypes

BF16 = ml_dtypes.bfloat16


def bf(x):
    return np.asarray(x, np.float32).astype(BF16)


def f32(x):
    return np.asarray(x, np.float32)


def f64(x):
    return np.asarray(x).astype(np.float64)


def striped(idx):
    return np.concatenate([l.reshape(-1, 16).T for l in idx])


def rows(idx, k):
    return np.tile(np.repeat(idx, 16, axis=0), (k // (16 * 8), 1))


def look(tab, idx):
    return np.take_along_axis(f64(tab), rows(idx, len(tab)), axis=1)


K, S, D, V, N = 256, 2048, 4, 512, 2048


def setup_inputs():
    return {"tab": f32(np.random.standard_normal((K, S))), "x0": f32(np.random.standard_normal((K, V))), "offs": striped(np.stack([np.random.permutation(S)[:N] for _ in range(8)]))}


def reference(tab, x0, offs):
    idx = np.stack([g.T.reshape(-1) for g in np.split(offs, 8)])
    x = f64(x0)
    for d in range(D):
        x = np.maximum(x, look(tab, idx[:, d * V:(d + 1) * V]))
    return x

@@ -1,0 +1,42 @@
+import concourse.mybir as mybir
+
+F32 = mybir.dt.float32
+U16 = mybir.dt.uint16
+MAX = mybir.AluOpType.max
+
+P = 128
+D = 4
+PER_COL = 16
+
+
+def tile_lookup_pool_max_out_kernel(tc, tab, x0, offs, out):
+    nc = tc.nc
+    rows, columns = tab.shape
+    width = x0.shape[1]
+    blocks = rows // P
+    piece = width // PER_COL
+
+    with (
+        tc.tile_pool(name="held", bufs=1) as held,
+        tc.tile_pool(name="running", bufs=2) as running,
+    ):
+        offsets = held.tile([P, D * piece], U16, name="offsets")
+        nc.sync.dma_start(offsets[:], offs)
+
+        windows, centres = [], []
+        for b in range(blocks):
+            window = held.tile([P, columns], F32, name=f"window{b}")
+            nc.sync.dma_start(window[:], tab[b * P : (b + 1) * P, :])
+            centre = held.tile([P, width], F32, name=f"centre{b}")
+            nc.sync.dma_start(centre[:], x0[b * P : (b + 1) * P, :])
+            windows.append(window)
+            centres.append(centre)
+
+        for b in range(blocks):
+            x = centres[b]
+            for d in range(D):
+                larger = running.tile([P, width], F32, name="larger")
+                picked = windows[b][:].indirect(offsets[:, d * piece : (d + 1) * piece])
+                nc.vector.tensor_tensor(larger[:], picked, x[:], MAX)
+                x = larger
+            nc.sync.dma_start(out[b * P : (b + 1) * P, :], x[:])

@@ -18,7 +18,7 @@ def tile_lookup_pool_max_out_kernel(tc, tab, x0, offs, out):
 
     with (
         tc.tile_pool(name="held", bufs=1) as held,
-        tc.tile_pool(name="running", bufs=2) as running,
+        tc.tile_pool(name="running", bufs=blocks * D) as running,
     ):
         offsets = held.tile([P, D * piece], U16, name="offsets")
         nc.sync.dma_start(offsets[:], offs)

@@ -23,20 +23,23 @@ def tile_lookup_pool_max_out_kernel(tc, tab, x0, offs, out):
         offsets = held.tile([P, D * piece], U16, name="offsets")
         nc.sync.dma_start(offsets[:], offs)
 
-        windows, centres = [], []
+        windows, x = [], []
         for b in range(blocks):
             window = held.tile([P, columns], F32, name=f"window{b}")
             nc.sync.dma_start(window[:], tab[b * P : (b + 1) * P, :])
             centre = held.tile([P, width], F32, name=f"centre{b}")
             nc.sync.dma_start(centre[:], x0[b * P : (b + 1) * P, :])
             windows.append(window)
-            centres.append(centre)
+            x.append(centre)
 
-        for b in range(blocks):
-            x = centres[b]
-            for d in range(D):
+        for step in range(D + blocks - 1):
+            for b in range(blocks):
+                d = step - b
+                if not 0 <= d < D:
+                    continue
                 larger = running.tile([P, width], F32, name="larger")
                 picked = windows[b][:].indirect(offsets[:, d * piece : (d + 1) * piece])
-                nc.vector.tensor_tensor(larger[:], picked, x[:], MAX)
-                x = larger
-            nc.sync.dma_start(out[b * P : (b + 1) * P, :], x[:])
+                nc.vector.tensor_tensor(larger[:], picked, x[b][:], MAX)
+                x[b] = larger
+                if d == D - 1:
+                    nc.sync.dma_start(out[b * P : (b + 1) * P, :], larger[:])

@@ -21,12 +21,13 @@ def tile_lookup_pool_max_out_kernel(tc, tab, x0, offs, out):
         tc.tile_pool(name="running", bufs=blocks * D) as running,
     ):
         offsets = held.tile([P, D * piece], U16, name="offsets")
-        nc.sync.dma_start(offsets[:], offs)
 
         windows, x = [], []
         for b in range(blocks):
             window = held.tile([P, columns], F32, name=f"window{b}")
             nc.sync.dma_start(window[:], tab[b * P : (b + 1) * P, :])
+            if b == 0:
+                nc.sync.dma_start(offsets[:], offs)
             centre = held.tile([P, width], F32, name=f"centre{b}")
             nc.sync.dma_start(centre[:], x0[b * P : (b + 1) * P, :])
             windows.append(window)

import concourse.mybir as mybir

F32 = mybir.dt.float32
U16 = mybir.dt.uint16
MAX = mybir.AluOpType.max

P = 128
D = 4
PER_COL = 16


def tile_lookup_pool_max_out_kernel(tc, tab, x0, offs, out):
    nc = tc.nc
    rows, columns = tab.shape
    width = x0.shape[1]
    blocks = rows // P
    piece = width // PER_COL

    with (
        tc.tile_pool(name="held", bufs=1) as held,
        tc.tile_pool(name="running", bufs=blocks * D) as running,
    ):
        offsets = held.tile([P, D * piece], U16, name="offsets")

        windows, x = [], []
        for b in range(blocks):
            window = held.tile([P, columns], F32, name=f"window{b}")
            nc.sync.dma_start(window[:], tab[b * P : (b + 1) * P, :])
            if b == 0:
                nc.sync.dma_start(offsets[:], offs)
            centre = held.tile([P, width], F32, name=f"centre{b}")
            nc.sync.dma_start(centre[:], x0[b * P : (b + 1) * P, :])
            windows.append(window)
            x.append(centre)

        for step in range(D + blocks - 1):
            for b in range(blocks):
                d = step - b
                if not 0 <= d < D:
                    continue
                larger = running.tile([P, width], F32, name="larger")
                picked = windows[b][:].indirect(offsets[:, d * piece : (d + 1) * piece])
                nc.vector.tensor_tensor(larger[:], picked, x[b][:], MAX)
                x[b] = larger
                if d == D - 1:
                    nc.sync.dma_start(out[b * P : (b + 1) * P, :], larger[:])
